import numpy as np
import ml_dtypes


def mxq(x, axis, fmt="e4m3"):
    dtype, down = {"e4m3": (ml_dtypes.float8_e4m3fn, 7), "e5m2": (ml_dtypes.float8_e5m2, 14)}[fmt]
    v = np.moveaxis(np.asarray(x, np.float32).astype(ml_dtypes.bfloat16).astype(np.float64), axis, -1)
    blocks = v.reshape(v.shape[:-1] + (-1, 32))
    amax = np.abs(blocks).max(-1, keepdims=True)
    byte = np.maximum(np.where(amax > 0, np.frexp(amax)[1] - 1 + 127, 0) - down, 1)
    scale = np.exp2(byte - 127.0)
    codes = (blocks / scale).astype(np.float32).astype(dtype).astype(np.float64)
    return np.moveaxis((codes * scale).reshape(v.shape), -1, axis)


WIDE = False


def mx_kscale(k):
    if not WIDE:
        return np.ones(k)
    levels = np.array([10, -10, 5, -5, 0])
    if k % 512:
        return np.exp2(np.random.permutation(np.resize(levels, k // 32))).repeat(32)
    a = np.empty((k // 512, 16))
    for p in range(k // 512):
        a[p, :8] = np.random.permutation(np.resize(levels, 8))
        for g in range(8):
            far = levels[np.abs(levels - a[p, g]) >= 10]
            a[p, g + 8] = far[np.random.randint(len(far))]
    return np.exp2(a.ravel()).repeat(32)


def f64(x):
    return np.asarray(x).astype(np.float64)


def striped(idx):
    return np.tile(idx.reshape(-1, 16).T, (8, 1)).astype(np.uint16)


def unstriped(offs):
    return offs[:16].T.reshape(-1).astype(np.int64)


def pack_weight(w):
    k, n = w.shape
    w = f64(np.asarray(w, np.float32).astype(ml_dtypes.bfloat16)).reshape(k // 32, 32, n)
    amax = np.abs(w).max(1)
    byte = np.clip(np.where(amax > 0, np.frexp(amax)[1] - 1 + 127 - 7, 1), 1, 254)
    scaled = (w * np.exp2(127.0 - byte)[:, None, :]).reshape(k, n).astype(np.float32)
    words = np.ascontiguousarray(scaled.reshape(k // 512, 128, 4, n).transpose(0, 1, 3, 2)).astype(ml_dtypes.float8_e4m3fn).view(np.uint8)
    return words, np.ascontiguousarray(byte.astype(np.uint8).reshape(k // 512, 16, n))


def unpack_weight(words, scales):
    g, p, n, _ = words.shape
    vals = np.ascontiguousarray(words).view(ml_dtypes.float8_e4m3fn).astype(np.float64) * np.repeat(np.exp2(scales.astype(np.float64) - 127.0), 8, axis=1)[..., None]
    return vals.transpose(0, 1, 3, 2).reshape(g * 512, n)


def sigmoid(v):
    return 1.0 / (1.0 + np.exp(-np.maximum(v, -700.0)))


K, T, S, H, W, N = 512, 2048, 512, 512, 2048, 512


def setup_inputs():
    n = np.random.standard_normal
    s = mx_kscale(K)[:, None]
    u = mx_kscale(H)
    packed_xT = pack_weight(n((K, T)) * s)
    packed_eT = pack_weight(n((K, W)) * s)
    return {
        "x_words": packed_xT[0],
        "x_scales": packed_xT[1],
        "e_words": packed_eT[0],
        "e_scales": packed_eT[1],
        "w1": (n((K, H)) / np.sqrt(2 * K) / s * u).astype(np.float32),
        "w2": (n((K, H)) / np.sqrt(2 * K) / s * u).astype(np.float32),
        "w3": (n((H, N)) / np.sqrt(H) / u[:, None]).astype(np.float32),
        "bias": (0.5 * n((N, 1))).astype(np.float32),
        "offs": striped(np.random.permutation(T)[:S]),
        "item": striped(np.random.permutation(W)[:S]),
    }


def reference(x_words, x_scales, e_words, e_scales, w1, w2, w3, bias, offs, item):
    xq = unpack_weight(x_words, x_scales)[:, unstriped(offs)]
    e_item = unpack_weight(e_words, e_scales)[:, unstriped(item)]
    y = mxq(f64(w1), 0, "e4m3").T @ xq + mxq(f64(w2), 0, "e4m3").T @ e_item
    rr = (mxq(f64(w3), 0, "e4m3").T @ mxq(y, 0, "e4m3")) + f64(bias)
    return y * sigmoid(rr) + y

@@ -1,0 +1,221 @@
+from contextlib import ExitStack
+
+import concourse.mybir as mybir
+
+K, T, S, H = 512, 2048, 512, 512
+FLOPS = 3 * 2 * 512 * 512 * 512
+
+F32 = mybir.dt.float32
+BF16 = mybir.dt.bfloat16
+I32 = mybir.dt.int32
+U32 = mybir.dt.uint32
+U16 = mybir.dt.uint16
+U8 = mybir.dt.uint8
+FP8X4 = mybir.dt.float8_e4m3fn_x4
+SIGMOID = mybir.ActivationFunctionType.Sigmoid
+ADD = mybir.AluOpType.add
+MULT = mybir.AluOpType.mult
+
+P = 128
+PACK = 4
+QUARTER = S // PACK
+E_ROW = 4
+W1_VECTOR_M = 48
+W2_VECTOR_M = 76
+W3_VECTOR_M = 24
+
+
+def tile_picked_ydcn_gate_p_kernel(
+    tc, x_words, x_scales, e_words, e_scales, w1, w2, w3, bias, offs, item, out
+):
+    nc = tc.nc
+    with ExitStack() as ctx:
+        keep = ctx.enter_context(tc.tile_pool(name="keep", bufs=1))
+        psum = ctx.enter_context(tc.psum_pool(name="psum", bufs=1))
+
+        def sb(name, shape, dtype):
+            return keep.tile(shape, dtype, name=name, align_bytes=64)
+
+        offs_list = keep.tile([P, S // 16], U16, name="offs_list")
+        item_list = keep.tile([P, S // 16], U16, name="item_list")
+        x_table = sb("x_table", [P, T], U32)
+        e_table = sb("e_table", [P, T], U32)
+        x_scale_table = sb("x_scale_table", [P, T], U8)
+        e_scale_table = sb("e_scale_table", [P, T], U8)
+        w_raw = [sb("w_raw%d" % n, [P, PACK, H], F32) for n in range(3)]
+        bias_sb = sb("bias_sb", [P, PACK], F32)
+
+        warm_in = sb("warm_in", [P, 1], F32)
+        warm_out = sb("warm_out", [P, 1], F32)
+        nc.vector.memset(x_scale_table[:].bitcast(I32), 0)
+        nc.vector.memset(e_scale_table[:].bitcast(I32), 0)
+        nc.vector.memset(warm_in[:], 0.0)
+
+        def load_weight(n, w):
+            nc.sync.dma_start(w_raw[n][:], w.rearrange("(p j) c -> p j c", j=PACK))
+
+        def load_words(table, words):
+            nc.sync.dma_start(table[:].bitcast(I32), words[0].rearrange("p n t -> p (n t)").bitcast(I32))
+
+        def load_scales(table, scales, row, queue):
+            for quad in range(4):
+                queue.dma_start(
+                    table[32 * quad + row : 32 * quad + row + 4, :].bitcast(I32),
+                    scales[0, 4 * quad : 4 * quad + 4, :].bitcast(I32),
+                )
+
+        nc.sync.dma_start(offs_list[:], offs)
+        load_scales(x_scale_table, x_scales, 0, nc.scalar)
+        nc.scalar.activation(warm_out[:], warm_in[:], SIGMOID)
+        load_weight(0, w1)
+        nc.sync.dma_start(item_list[:], item)
+        load_words(x_table, x_words)
+        load_scales(e_scale_table, e_scales, E_ROW, nc.sync)
+        load_weight(1, w2)
+        load_words(e_table, e_words)
+        load_weight(2, w3)
+        nc.sync.dma_start(bias_sb[:], bias.rearrange("(p t) o -> p (t o)", t=PACK))
+
+        w_bf = [sb("w_bf%d" % n, [P, PACK, P, PACK], BF16) for n in range(2)]
+        w_codes = [sb("w_codes%d" % n, [P, H], U32) for n in range(2)]
+        w_scale = [sb("w_scale%d" % n, [P, H], U8) for n in range(2)]
+
+        def cast_weight(n, vector_m):
+            src = w_raw[n][:].rearrange("p j (m t) -> p m t j", t=PACK)
+            dst = w_bf[n][:].rearrange("p t m j -> p m t j")
+            if vector_m > 0:
+                nc.vector.tensor_copy(dst[:, :vector_m], src[:, :vector_m])
+            nc.scalar.copy(dst[:, vector_m:], src[:, vector_m:])
+
+        def quantize_weight(n):
+            nc.vector.quantize_mx(
+                out=w_codes[n][:].bitcast(FP8X4),
+                scales=w_scale[n][:],
+                in_=w_bf[n][:].rearrange("p t m j -> p (t m j)"),
+            )
+
+        x_codes = sb("x_codes", [P, S], U32)
+        x_scale = sb("x_scale", [P, S], U8)
+        e_scale = sb("e_scale", [P, S], U8)
+        e_codes = [sb("e_codes%d" % half, [P, S // 2], U32) for half in range(2)]
+
+        cast_weight(0, W1_VECTOR_M)
+        nc.vector.tensor_copy(x_scale[:], x_scale_table[:].indirect(offs_list[:]))
+        nc.vector.tensor_copy(e_scale[:], e_scale_table[:].indirect(item_list[:]))
+        nc.vector.tensor_copy(x_codes[:], x_table[:].indirect(offs_list[:]))
+        quantize_weight(0)
+
+        y_bank = [psum.tile([P, PACK, QUARTER], F32, name="y_bank%d" % q) for q in range(PACK)]
+        r_bank = [psum.tile([P, S], F32, name="r_bank%d" % t) for t in range(PACK)]
+
+        def x_pass(q, t, start):
+            rows = slice(t * P, (t + 1) * P)
+            cols = slice(q * QUARTER, (q + 1) * QUARTER)
+            nc.tensor.matmul_mx(
+                out=y_bank[q][:, t, :],
+                lhsT=w_codes[0][:, rows].bitcast(FP8X4),
+                lhsT_scale=w_scale[0][:, rows],
+                rhs=x_codes[:, cols].bitcast(FP8X4),
+                rhs_scale=x_scale[:, cols],
+                start=start,
+                stop=False,
+            )
+
+        def e_pass(q, t, stop):
+            rows = slice(t * P, (t + 1) * P)
+            cols = slice(q * QUARTER, (q + 1) * QUARTER)
+            within = slice((q % 2) * QUARTER, (q % 2 + 1) * QUARTER)
+            nc.tensor.matmul_mx(
+                out=y_bank[q][:, t, :],
+                lhsT=w_codes[1][:, rows].bitcast(FP8X4),
+                lhsT_scale=w_scale[1][:, rows],
+                rhs=e_codes[q // 2][:, within].bitcast(FP8X4),
+                rhs_scale=e_scale[E_ROW:P, cols],
+                start=False,
+                stop=stop,
+            )
+
+        for q in range(PACK):
+            for t in range(PACK):
+                x_pass(q, t, t == 0)
+
+        cast_weight(1, W2_VECTOR_M)
+        quantize_weight(1)
+
+        for half in range(2):
+            nc.vector.tensor_copy(e_codes[half][:], e_table[:].indirect(item_list[:, 16 * half : 16 * half + 16]))
+
+        y_bf = [sb("y_bf%d" % q, [P, QUARTER, PACK], BF16) for q in range(PACK)]
+        y_codes = sb("y_codes", [P, S], U32)
+        y_scale = sb("y_scale", [P, S], U8)
+        for q in range(PACK):
+            for t in range(PACK):
+                e_pass(q, t, t == PACK - 1)
+
+            turned = y_bank[q][:].rearrange("p t n -> p n t")
+            if q == 1:
+                nc.vector.tensor_copy(y_bf[q][:], turned)
+            else:
+                nc.scalar.copy(y_bf[q][:], turned)
+
+        def quantize_y(q):
+            cols = slice(q * QUARTER, (q + 1) * QUARTER)
+            nc.vector.quantize_mx(
+                out=y_codes[:, cols].bitcast(FP8X4),
+                scales=y_scale[:, cols],
+                in_=y_bf[q][:].rearrange("p n t -> p (n t)"),
+            )
+
+        quantize_y(0)
+        quantize_y(1)
+
+        w3_bf = [sb("w3_bf%d" % u, [P, 2, P, PACK], BF16) for u in range(2)]
+        w3_codes = [sb("w3_codes%d" % t, [P, P], U32) for t in range(PACK)]
+        w3_scale = [sb("w3_scale%d" % t, [P, P], U8) for t in range(PACK)]
+        w3_src = w_raw[2][:].rearrange("p j (m t) -> p m j t", t=PACK)
+
+        def w3_views(u):
+            return w3_bf[u][:].rearrange("p t m j -> p m j t"), w3_src[:, :, :, 2 * u : 2 * u + 2]
+
+        def quantize_w3(t):
+            nc.vector.quantize_mx(
+                out=w3_codes[t][:].bitcast(FP8X4),
+                scales=w3_scale[t][:],
+                in_=w3_bf[t // 2][:, t % 2].rearrange("p m j -> p (m j)"),
+            )
+
+        dst, src = w3_views(0)
+        nc.vector.tensor_copy(dst, src)
+        dst, src = w3_views(1)
+        nc.scalar.copy(dst[:, W3_VECTOR_M:], src[:, W3_VECTOR_M:])
+        quantize_y(2)
+        quantize_y(3)
+        quantize_w3(0)
+        quantize_w3(1)
+        nc.vector.tensor_copy(dst[:, :W3_VECTOR_M], src[:, :W3_VECTOR_M])
+        quantize_w3(2)
+        quantize_w3(3)
+
+        out_rows = out.rearrange("(p t) j -> p t j", t=PACK)
+        for t in range(PACK):
+            nc.tensor.matmul_mx(
+                out=r_bank[t][:],
+                lhsT=w3_codes[t][:].bitcast(FP8X4),
+                lhsT_scale=w3_scale[t][:],
+                rhs=y_codes[:].bitcast(FP8X4),
+                rhs_scale=y_scale[:],
+                start=True,
+                stop=True,
+            )
+            pieces = 2 if t == PACK - 1 else 1
+            width = S // pieces
+            for piece in range(pieces):
+                span = slice(piece * width, (piece + 1) * width)
+                gate = sb("gate%d_%d" % (t, piece), [P, width], F32)
+                result = sb("result%d_%d" % (t, piece), [P, width], F32)
+                nc.scalar.activation(gate[:], r_bank[t][:, span], SIGMOID, bias=bias_sb[:, t : t + 1])
+                for n in range(width // QUARTER):
+                    q = piece * (width // QUARTER) + n
+                    cols = slice(n * QUARTER, (n + 1) * QUARTER)
+                    nc.vector.scalar_tensor_tensor(result[:, cols], gate[:, cols], 1.0, y_bank[q][:, t, :], ADD, MULT)
+                nc.sync.dma_start(out_rows[:, t, span], result[:])

@@ -20,9 +20,9 @@ P = 128
 PACK = 4
 QUARTER = S // PACK
 E_ROW = 4
-W1_VECTOR_M = 48
-W2_VECTOR_M = 76
-W3_VECTOR_M = 24
+W1_VECTOR_M = 84
+W2_VECTOR_M = 66
+W3_VECTOR_M = 32
 
 
 def tile_picked_ydcn_gate_p_kernel(
@@ -64,12 +64,12 @@ def tile_picked_ydcn_gate_p_kernel(
                     scales[0, 4 * quad : 4 * quad + 4, :].bitcast(I32),
                 )
 
-        nc.sync.dma_start(offs_list[:], offs)
-        load_scales(x_scale_table, x_scales, 0, nc.scalar)
-        nc.scalar.activation(warm_out[:], warm_in[:], SIGMOID)
         load_weight(0, w1)
-        nc.sync.dma_start(item_list[:], item)
+        load_scales(x_scale_table, x_scales, 0, nc.sync)
+        nc.scalar.activation(warm_out[:], warm_in[:], SIGMOID)
+        nc.sync.dma_start(offs_list[:], offs)
         load_words(x_table, x_words)
+        nc.sync.dma_start(item_list[:], item)
         load_scales(e_scale_table, e_scales, E_ROW, nc.sync)
         load_weight(1, w2)
         load_words(e_table, e_words)
@@ -141,33 +141,40 @@ def tile_picked_ydcn_gate_p_kernel(
 
         cast_weight(1, W2_VECTOR_M)
         quantize_weight(1)
+        for t in range(3):
+            rows = slice(t * P, (t + 1) * P)
+            nc.tensor.matmul_mx(
+                out=r_bank[t][:],
+                lhsT=w_codes[1][:, rows].bitcast(FP8X4),
+                lhsT_scale=w_scale[1][:, rows],
+                rhs=x_codes[:].bitcast(FP8X4),
+                rhs_scale=x_scale[:],
+                start=True,
+                stop=True,
+            )
 
         for half in range(2):
             nc.vector.tensor_copy(e_codes[half][:], e_table[:].indirect(item_list[:, 16 * half : 16 * half + 16]))
 
-        y_bf = [sb("y_bf%d" % q, [P, QUARTER, PACK], BF16) for q in range(PACK)]
+        y_bf = [sb("y_bf%d" % half, [P, 2, QUARTER, PACK], BF16) for half in range(2)]
         y_codes = sb("y_codes", [P, S], U32)
         y_scale = sb("y_scale", [P, S], U8)
         for q in range(PACK):
             for t in range(PACK):
                 e_pass(q, t, t == PACK - 1)
-
             turned = y_bank[q][:].rearrange("p t n -> p n t")
-            if q == 1:
-                nc.vector.tensor_copy(y_bf[q][:], turned)
+            if q in (0, 2):
+                nc.vector.tensor_copy(y_bf[q // 2][:, q % 2], turned)
             else:
-                nc.scalar.copy(y_bf[q][:], turned)
+                nc.scalar.copy(y_bf[q // 2][:, q % 2], turned)
 
-        def quantize_y(q):
-            cols = slice(q * QUARTER, (q + 1) * QUARTER)
+        def quantize_y(half):
+            cols = slice(half * (S // 2), (half + 1) * (S // 2))
             nc.vector.quantize_mx(
                 out=y_codes[:, cols].bitcast(FP8X4),
                 scales=y_scale[:, cols],
-                in_=y_bf[q][:].rearrange("p n t -> p (n t)"),
+                in_=y_bf[half][:].rearrange("p q n t -> p (q n t)"),
             )
-
-        quantize_y(0)
-        quantize_y(1)
 
         w3_bf = [sb("w3_bf%d" % u, [P, 2, P, PACK], BF16) for u in range(2)]
         w3_codes = [sb("w3_codes%d" % t, [P, P], U32) for t in range(PACK)]
@@ -184,19 +191,19 @@ def tile_picked_ydcn_gate_p_kernel(
                 in_=w3_bf[t // 2][:, t % 2].rearrange("p m j -> p (m j)"),
             )
 
+        quantize_y(0)
+        quantize_y(1)
         dst, src = w3_views(0)
-        nc.vector.tensor_copy(dst, src)
+        nc.vector.tensor_copy(dst[:, :56], src[:, :56])
+        nc.scalar.copy(dst[:, 56:], src[:, 56:])
         dst, src = w3_views(1)
         nc.scalar.copy(dst[:, W3_VECTOR_M:], src[:, W3_VECTOR_M:])
-        quantize_y(2)
-        quantize_y(3)
         quantize_w3(0)
         quantize_w3(1)
         nc.vector.tensor_copy(dst[:, :W3_VECTOR_M], src[:, :W3_VECTOR_M])
         quantize_w3(2)
         quantize_w3(3)
 
-        out_rows = out.rearrange("(p t) j -> p t j", t=PACK)
         for t in range(PACK):
             nc.tensor.matmul_mx(
                 out=r_bank[t][:],
@@ -207,15 +214,21 @@ def tile_picked_ydcn_gate_p_kernel(
                 start=True,
                 stop=True,
             )
-            pieces = 2 if t == PACK - 1 else 1
+
+        out_rows = out.rearrange("(p t) j -> p t j", t=PACK)
+        for u, pieces in enumerate((2, 2)):
             width = S // pieces
             for piece in range(pieces):
                 span = slice(piece * width, (piece + 1) * width)
-                gate = sb("gate%d_%d" % (t, piece), [P, width], F32)
-                result = sb("result%d_%d" % (t, piece), [P, width], F32)
-                nc.scalar.activation(gate[:], r_bank[t][:, span], SIGMOID, bias=bias_sb[:, t : t + 1])
+                gate = sb("gate%d_%d" % (u, piece), [P, 2, width], F32)
+                result = sb("result%d_%d" % (u, piece), [P, 2, width], F32)
+                for n in range(2):
+                    t = 2 * u + n
+                    nc.scalar.activation(gate[:, n, :], r_bank[t][:, span], SIGMOID, bias=bias_sb[:, t : t + 1])
                 for n in range(width // QUARTER):
                     q = piece * (width // QUARTER) + n
                     cols = slice(n * QUARTER, (n + 1) * QUARTER)
-                    nc.vector.scalar_tensor_tensor(result[:, cols], gate[:, cols], 1.0, y_bank[q][:, t, :], ADD, MULT)
-                nc.sync.dma_start(out_rows[:, t, span], result[:])
+                    nc.vector.scalar_tensor_tensor(
+                        result[:, :, cols], gate[:, :, cols], 1.0, y_bank[q][:, 2 * u : 2 * u + 2, :], ADD, MULT
+                    )
+                nc.sync.dma_start(out_rows[:, 2 * u : 2 * u + 2, span], result[:])

@@ -58,10 +58,10 @@ def tile_picked_ydcn_gate_p_kernel(
             nc.sync.dma_start(table[:].bitcast(I32), words[0].rearrange("p n t -> p (n t)").bitcast(I32))
 
         def load_scales(table, scales, row, queue):
-            for quad in range(4):
+            for r in range(4):
                 queue.dma_start(
-                    table[32 * quad + row : 32 * quad + row + 4, :].bitcast(I32),
-                    scales[0, 4 * quad : 4 * quad + 4, :].bitcast(I32),
+                    table[row + r : P : 32, :].bitcast(I32),
+                    scales[0, r:16:4, :].bitcast(I32),
                 )
 
         load_weight(0, w1)

@@ -19,10 +19,9 @@ MULT = mybir.AluOpType.mult
 P = 128
 PACK = 4
 QUARTER = S // PACK
-E_ROW = 4
-W1_VECTOR_M = 84
-W2_VECTOR_M = 66
-W3_VECTOR_M = 32
+HALF = S // 2
+SPREAD = 8
+W_VECTOR_M = (32, 64)
 
 
 def tile_picked_ydcn_gate_p_kernel(
@@ -33,8 +32,8 @@ def tile_picked_ydcn_gate_p_kernel(
         keep = ctx.enter_context(tc.tile_pool(name="keep", bufs=1))
         psum = ctx.enter_context(tc.psum_pool(name="psum", bufs=1))
 
-        def sb(name, shape, dtype):
-            return keep.tile(shape, dtype, name=name, align_bytes=64)
+        def sb(name, shape, dtype, tag=None):
+            return keep.tile(shape, dtype, name=name, tag=tag or name, align_bytes=64)
 
         offs_list = keep.tile([P, S // 16], U16, name="offs_list")
         item_list = keep.tile([P, S // 16], U16, name="item_list")
@@ -47,45 +46,48 @@ def tile_picked_ydcn_gate_p_kernel(
 
         warm_in = sb("warm_in", [P, 1], F32)
         warm_out = sb("warm_out", [P, 1], F32)
+        picked_scale = sb("picked_scale", [P, 2 * S], U8)
+        scale = sb("scale", [P, 2 * S], U8)
         nc.vector.memset(x_scale_table[:].bitcast(I32), 0)
         nc.vector.memset(e_scale_table[:].bitcast(I32), 0)
         nc.vector.memset(warm_in[:], 0.0)
+        nc.vector.memset(scale[:].bitcast(I32), 0)
+        nc.scalar.activation(warm_out[:], warm_in[:], SIGMOID)
 
-        def load_weight(n, w):
-            nc.sync.dma_start(w_raw[n][:], w.rearrange("(p j) c -> p j c", j=PACK))
+        def load_weight(n, w, rows):
+            nc.sync.dma_start(w_raw[n][:, rows], w.rearrange("(p j) c -> p j c", j=PACK)[:, rows])
 
         def load_words(table, words):
             nc.sync.dma_start(table[:].bitcast(I32), words[0].rearrange("p n t -> p (n t)").bitcast(I32))
 
-        def load_scales(table, scales, row, queue):
-            for r in range(4):
-                queue.dma_start(
-                    table[row + r : P : 32, :].bitcast(I32),
-                    scales[0, r:16:4, :].bitcast(I32),
-                )
+        def load_scales(table, scales):
+            nc.sync.dma_start(table[0:P:SPREAD, :].bitcast(I32), scales[0].bitcast(I32))
 
-        load_weight(0, w1)
-        load_scales(x_scale_table, x_scales, 0, nc.sync)
-        nc.scalar.activation(warm_out[:], warm_in[:], SIGMOID)
+        load_weight(0, w1, slice(0, 2))
         nc.sync.dma_start(offs_list[:], offs)
-        load_words(x_table, x_words)
         nc.sync.dma_start(item_list[:], item)
-        load_scales(e_scale_table, e_scales, E_ROW, nc.sync)
-        load_weight(1, w2)
+        load_scales(x_scale_table, x_scales)
+        load_scales(e_scale_table, e_scales)
+        load_weight(0, w1, slice(2, 4))
+        load_words(x_table, x_words)
+        load_weight(1, w2, slice(0, 4))
+        nc.vector.tensor_copy(picked_scale[:, :S], x_scale_table[:].indirect(offs_list[:]))
+        nc.vector.tensor_copy(picked_scale[:, S:], e_scale_table[:].indirect(item_list[:]))
+        for r in range(4):
+            nc.sync.dma_start(scale[r:P:32, :].bitcast(I32), picked_scale[SPREAD * r : P : 32, :].bitcast(I32))
         load_words(e_table, e_words)
-        load_weight(2, w3)
+        load_weight(2, w3, slice(0, 4))
         nc.sync.dma_start(bias_sb[:], bias.rearrange("(p t) o -> p (t o)", t=PACK))
 
         w_bf = [sb("w_bf%d" % n, [P, PACK, P, PACK], BF16) for n in range(2)]
         w_codes = [sb("w_codes%d" % n, [P, H], U32) for n in range(2)]
         w_scale = [sb("w_scale%d" % n, [P, H], U8) for n in range(2)]
 
-        def cast_weight(n, vector_m):
+        def cast_weight(n):
             src = w_raw[n][:].rearrange("p j (m t) -> p m t j", t=PACK)
             dst = w_bf[n][:].rearrange("p t m j -> p m t j")
-            if vector_m > 0:
-                nc.vector.tensor_copy(dst[:, :vector_m], src[:, :vector_m])
-            nc.scalar.copy(dst[:, vector_m:], src[:, vector_m:])
+            nc.vector.tensor_copy(dst[:, : W_VECTOR_M[n]], src[:, : W_VECTOR_M[n]])
+            nc.scalar.copy(dst[:, W_VECTOR_M[n] :], src[:, W_VECTOR_M[n] :])
 
         def quantize_weight(n):
             nc.vector.quantize_mx(
@@ -94,141 +96,106 @@ def tile_picked_ydcn_gate_p_kernel(
                 in_=w_bf[n][:].rearrange("p t m j -> p (t m j)"),
             )
 
-        x_codes = sb("x_codes", [P, S], U32)
-        x_scale = sb("x_scale", [P, S], U8)
-        e_scale = sb("e_scale", [P, S], U8)
-        e_codes = [sb("e_codes%d" % half, [P, S // 2], U32) for half in range(2)]
+        x_codes = [sb("x_codes%d" % half, [P, HALF], U32) for half in range(2)]
+        e_codes = [sb("e_codes%d" % half, [P, HALF], U32) for half in range(2)]
 
-        cast_weight(0, W1_VECTOR_M)
-        nc.vector.tensor_copy(x_scale[:], x_scale_table[:].indirect(offs_list[:]))
-        nc.vector.tensor_copy(e_scale[:], e_scale_table[:].indirect(item_list[:]))
-        nc.vector.tensor_copy(x_codes[:], x_table[:].indirect(offs_list[:]))
+        cast_weight(0)
         quantize_weight(0)
 
         y_bank = [psum.tile([P, PACK, QUARTER], F32, name="y_bank%d" % q) for q in range(PACK)]
-        r_bank = [psum.tile([P, S], F32, name="r_bank%d" % t) for t in range(PACK)]
+        r_bank = [[psum.tile([P, 2, HALF], F32, name="r_bank%d_%d" % (u, half)) for half in range(2)] for u in range(2)]
 
-        def x_pass(q, t, start):
+        def first_pass(n, codes, q, t):
             rows = slice(t * P, (t + 1) * P)
-            cols = slice(q * QUARTER, (q + 1) * QUARTER)
-            nc.tensor.matmul_mx(
-                out=y_bank[q][:, t, :],
-                lhsT=w_codes[0][:, rows].bitcast(FP8X4),
-                lhsT_scale=w_scale[0][:, rows],
-                rhs=x_codes[:, cols].bitcast(FP8X4),
-                rhs_scale=x_scale[:, cols],
-                start=start,
-                stop=False,
-            )
-
-        def e_pass(q, t, stop):
-            rows = slice(t * P, (t + 1) * P)
-            cols = slice(q * QUARTER, (q + 1) * QUARTER)
             within = slice((q % 2) * QUARTER, (q % 2 + 1) * QUARTER)
             nc.tensor.matmul_mx(
                 out=y_bank[q][:, t, :],
-                lhsT=w_codes[1][:, rows].bitcast(FP8X4),
-                lhsT_scale=w_scale[1][:, rows],
-                rhs=e_codes[q // 2][:, within].bitcast(FP8X4),
-                rhs_scale=e_scale[E_ROW:P, cols],
-                start=False,
-                stop=stop,
+                lhsT=w_codes[n][:, rows].bitcast(FP8X4),
+                lhsT_scale=w_scale[n][:, rows],
+                rhs=codes[q // 2][:, within].bitcast(FP8X4),
+                rhs_scale=scale[:, n * S + q * QUARTER : n * S + (q + 1) * QUARTER],
+                start=(n == 0 and t == 0),
+                stop=(n == 1 and t == PACK - 1),
             )
 
+        for half in range(2):
+            nc.vector.tensor_copy(x_codes[half][:], x_table[:].indirect(offs_list[:, 16 * half : 16 * half + 16]))
         for q in range(PACK):
             for t in range(PACK):
-                x_pass(q, t, t == 0)
+                first_pass(0, x_codes, q, t)
 
-        cast_weight(1, W2_VECTOR_M)
+        cast_weight(1)
         quantize_weight(1)
-        for t in range(3):
-            rows = slice(t * P, (t + 1) * P)
-            nc.tensor.matmul_mx(
-                out=r_bank[t][:],
-                lhsT=w_codes[1][:, rows].bitcast(FP8X4),
-                lhsT_scale=w_scale[1][:, rows],
-                rhs=x_codes[:].bitcast(FP8X4),
-                rhs_scale=x_scale[:],
-                start=True,
-                stop=True,
-            )
 
         for half in range(2):
             nc.vector.tensor_copy(e_codes[half][:], e_table[:].indirect(item_list[:, 16 * half : 16 * half + 16]))
 
         y_bf = [sb("y_bf%d" % half, [P, 2, QUARTER, PACK], BF16) for half in range(2)]
-        y_codes = sb("y_codes", [P, S], U32)
-        y_scale = sb("y_scale", [P, S], U8)
+        y_codes = [sb("y_codes%d" % half, [P, HALF], U32) for half in range(2)]
+        w3_bf = [sb("w3_bf%d" % u, [P, 2, P, PACK], BF16) for u in range(2)]
+        y_scale = [sb("y_scale0", [P, HALF], U8)]
         for q in range(PACK):
             for t in range(PACK):
-                e_pass(q, t, t == PACK - 1)
+                first_pass(1, e_codes, q, t)
             turned = y_bank[q][:].rearrange("p t n -> p n t")
-            if q in (0, 2):
+            if q == 1:
                 nc.vector.tensor_copy(y_bf[q // 2][:, q % 2], turned)
             else:
                 nc.scalar.copy(y_bf[q // 2][:, q % 2], turned)
 
         def quantize_y(half):
-            cols = slice(half * (S // 2), (half + 1) * (S // 2))
             nc.vector.quantize_mx(
-                out=y_codes[:, cols].bitcast(FP8X4),
-                scales=y_scale[:, cols],
+                out=y_codes[half][:].bitcast(FP8X4),
+                scales=y_scale[half][:],
                 in_=y_bf[half][:].rearrange("p q n t -> p (q n t)"),
             )
 
-        w3_bf = [sb("w3_bf%d" % u, [P, 2, P, PACK], BF16) for u in range(2)]
-        w3_codes = [sb("w3_codes%d" % t, [P, P], U32) for t in range(PACK)]
-        w3_scale = [sb("w3_scale%d" % t, [P, P], U8) for t in range(PACK)]
+        w3_codes = [sb("w3_codes%d" % u, [P, 2 * P], U32) for u in range(2)]
+        w3_scale = [sb("w3_scale%d" % u, [P, 2 * P], U8) for u in range(2)]
         w3_src = w_raw[2][:].rearrange("p j (m t) -> p m j t", t=PACK)
 
         def w3_views(u):
             return w3_bf[u][:].rearrange("p t m j -> p m j t"), w3_src[:, :, :, 2 * u : 2 * u + 2]
 
-        def quantize_w3(t):
+        def quantize_w3(u):
             nc.vector.quantize_mx(
-                out=w3_codes[t][:].bitcast(FP8X4),
-                scales=w3_scale[t][:],
-                in_=w3_bf[t // 2][:, t % 2].rearrange("p m j -> p (m j)"),
+                out=w3_codes[u][:].bitcast(FP8X4),
+                scales=w3_scale[u][:],
+                in_=w3_bf[u][:].rearrange("p t m j -> p (t m j)"),
             )
 
-        quantize_y(0)
-        quantize_y(1)
         dst, src = w3_views(0)
-        nc.vector.tensor_copy(dst[:, :56], src[:, :56])
-        nc.scalar.copy(dst[:, 56:], src[:, 56:])
-        dst, src = w3_views(1)
-        nc.scalar.copy(dst[:, W3_VECTOR_M:], src[:, W3_VECTOR_M:])
+        nc.vector.tensor_copy(dst, src)
+        quantize_y(0)
         quantize_w3(0)
+        y_scale.append(sb("y_scale1", [P, HALF], U8, "w3_bf0"))
+        quantize_y(1)
+        dst, src = w3_views(1)
+        nc.scalar.copy(dst, src)
         quantize_w3(1)
-        nc.vector.tensor_copy(dst[:, :W3_VECTOR_M], src[:, :W3_VECTOR_M])
-        quantize_w3(2)
-        quantize_w3(3)
-
-        for t in range(PACK):
-            nc.tensor.matmul_mx(
-                out=r_bank[t][:],
-                lhsT=w3_codes[t][:].bitcast(FP8X4),
-                lhsT_scale=w3_scale[t][:],
-                rhs=y_codes[:].bitcast(FP8X4),
-                rhs_scale=y_scale[:],
-                start=True,
-                stop=True,
-            )
 
         out_rows = out.rearrange("(p t) j -> p t j", t=PACK)
-        for u, pieces in enumerate((2, 2)):
-            width = S // pieces
-            for piece in range(pieces):
-                span = slice(piece * width, (piece + 1) * width)
-                gate = sb("gate%d_%d" % (u, piece), [P, 2, width], F32)
-                result = sb("result%d_%d" % (u, piece), [P, 2, width], F32)
+        for u in range(2):
+            for half in range(2):
+                for n in range(2):
+                    rows = slice(n * P, (n + 1) * P)
+                    nc.tensor.matmul_mx(
+                        out=r_bank[u][half][:, n, :],
+                        lhsT=w3_codes[u][:, rows].bitcast(FP8X4),
+                        lhsT_scale=w3_scale[u][:, rows],
+                        rhs=y_codes[half][:].bitcast(FP8X4),
+                        rhs_scale=y_scale[half][:],
+                        start=True,
+                        stop=True,
+                    )
+                gate = sb("gate%d_%d" % (u, half), [P, 2, HALF], F32)
+                result = sb("result%d_%d" % (u, half), [P, 2, HALF], F32)
                 for n in range(2):
                     t = 2 * u + n
-                    nc.scalar.activation(gate[:, n, :], r_bank[t][:, span], SIGMOID, bias=bias_sb[:, t : t + 1])
-                for n in range(width // QUARTER):
-                    q = piece * (width // QUARTER) + n
+                    nc.scalar.activation(gate[:, n, :], r_bank[u][half][:, n, :], SIGMOID, bias=bias_sb[:, t : t + 1])
+                for n in range(2):
                     cols = slice(n * QUARTER, (n + 1) * QUARTER)
                     nc.vector.scalar_tensor_tensor(
-                        result[:, :, cols], gate[:, :, cols], 1.0, y_bank[q][:, 2 * u : 2 * u + 2, :], ADD, MULT
+                        result[:, :, cols], gate[:, :, cols], 1.0, y_bank[2 * half + n][:, 2 * u : 2 * u + 2, :], ADD, MULT
                     )
-                nc.sync.dma_start(out_rows[:, 2 * u : 2 * u + 2, span], result[:])
+                nc.sync.dma_start(out_rows[:, 2 * u : 2 * u + 2, half * HALF : (half + 1) * HALF], result[:])

@@ -41,7 +41,8 @@ def tile_picked_ydcn_gate_p_kernel(
         e_table = sb("e_table", [P, T], U32)
         x_scale_table = sb("x_scale_table", [P, T], U8)
         e_scale_table = sb("e_scale_table", [P, T], U8)
-        w_raw = [sb("w_raw%d" % n, [P, PACK, H], F32) for n in range(3)]
+        w_raw = [sb("w_raw%d" % n, [P, PACK, H], F32) for n in range(2)]
+        w3_raw = [sb("w3_raw%d" % side, [P, PACK, H // 2], F32) for side in range(2)]
         bias_sb = sb("bias_sb", [P, PACK], F32)
 
         warm_in = sb("warm_in", [P, 1], F32)
@@ -76,7 +77,9 @@ def tile_picked_ydcn_gate_p_kernel(
         for r in range(4):
             nc.sync.dma_start(scale[r:P:32, :].bitcast(I32), picked_scale[SPREAD * r : P : 32, :].bitcast(I32))
         load_words(e_table, e_words)
-        load_weight(2, w3, slice(0, 4))
+        for side in range(2):
+            cols = slice(side * (H // 2), (side + 1) * (H // 2))
+            nc.sync.dma_start(w3_raw[side][:], w3.rearrange("(p j) c -> p j c", j=PACK)[:, :, cols])
         nc.sync.dma_start(bias_sb[:], bias.rearrange("(p t) o -> p (t o)", t=PACK))
 
         w_bf = [sb("w_bf%d" % n, [P, PACK, P, PACK], BF16) for n in range(2)]
@@ -103,7 +106,6 @@ def tile_picked_ydcn_gate_p_kernel(
         quantize_weight(0)
 
         y_bank = [psum.tile([P, PACK, QUARTER], F32, name="y_bank%d" % q) for q in range(PACK)]
-        r_bank = [[psum.tile([P, 2, HALF], F32, name="r_bank%d_%d" % (u, half)) for half in range(2)] for u in range(2)]
 
         def first_pass(n, codes, q, t):
             rows = slice(t * P, (t + 1) * P)
@@ -133,15 +135,12 @@ def tile_picked_ydcn_gate_p_kernel(
         y_bf = [sb("y_bf%d" % half, [P, 2, QUARTER, PACK], BF16) for half in range(2)]
         y_codes = [sb("y_codes%d" % half, [P, HALF], U32) for half in range(2)]
         w3_bf = [sb("w3_bf%d" % u, [P, 2, P, PACK], BF16) for u in range(2)]
-        y_scale = [sb("y_scale0", [P, HALF], U8)]
+        y_scale = []
         for q in range(PACK):
             for t in range(PACK):
                 first_pass(1, e_codes, q, t)
             turned = y_bank[q][:].rearrange("p t n -> p n t")
-            if q == 1:
-                nc.vector.tensor_copy(y_bf[q // 2][:, q % 2], turned)
-            else:
-                nc.scalar.copy(y_bf[q // 2][:, q % 2], turned)
+            nc.scalar.copy(y_bf[q // 2][:, q % 2], turned)
 
         def quantize_y(half):
             nc.vector.quantize_mx(
@@ -152,10 +151,11 @@ def tile_picked_ydcn_gate_p_kernel(
 
         w3_codes = [sb("w3_codes%d" % u, [P, 2 * P], U32) for u in range(2)]
         w3_scale = [sb("w3_scale%d" % u, [P, 2 * P], U8) for u in range(2)]
-        w3_src = w_raw[2][:].rearrange("p j (m t) -> p m j t", t=PACK)
 
-        def w3_views(u):
-            return w3_bf[u][:].rearrange("p t m j -> p m j t"), w3_src[:, :, :, 2 * u : 2 * u + 2]
+        def cast_w3(side, u):
+            dst = w3_bf[u][:].rearrange("p t m j -> p m j t")[:, side * (P // 2) : (side + 1) * (P // 2)]
+            src = w3_raw[side][:].rearrange("p j (m t) -> p m j t", t=PACK)[:, :, :, 2 * u : 2 * u + 2]
+            nc.vector.tensor_copy(dst, src)
 
         def quantize_w3(u):
             nc.vector.quantize_mx(
@@ -164,38 +164,51 @@ def tile_picked_ydcn_gate_p_kernel(
                 in_=w3_bf[u][:].rearrange("p t m j -> p (t m j)"),
             )
 
-        dst, src = w3_views(0)
-        nc.vector.tensor_copy(dst, src)
-        quantize_y(0)
+        for side in range(2):
+            for u in range(2):
+                cast_w3(side, u)
         quantize_w3(0)
-        y_scale.append(sb("y_scale1", [P, HALF], U8, "w3_bf0"))
-        quantize_y(1)
-        dst, src = w3_views(1)
-        nc.scalar.copy(dst, src)
+        y_scale.append(sb("y_scale0", [P, HALF], U8, "w3_raw1"))
+        quantize_y(0)
         quantize_w3(1)
+        y_scale.append(sb("y_scale1", [P, HALF], U8, "y_bf0"))
+        quantize_y(1)
 
         out_rows = out.rearrange("(p t) j -> p t j", t=PACK)
-        for u in range(2):
-            for half in range(2):
-                for n in range(2):
-                    rows = slice(n * P, (n + 1) * P)
-                    nc.tensor.matmul_mx(
-                        out=r_bank[u][half][:, n, :],
-                        lhsT=w3_codes[u][:, rows].bitcast(FP8X4),
-                        lhsT_scale=w3_scale[u][:, rows],
-                        rhs=y_codes[half][:].bitcast(FP8X4),
-                        rhs_scale=y_scale[half][:],
-                        start=True,
-                        stop=True,
-                    )
-                gate = sb("gate%d_%d" % (u, half), [P, 2, HALF], F32)
-                result = sb("result%d_%d" % (u, half), [P, 2, HALF], F32)
-                for n in range(2):
-                    t = 2 * u + n
-                    nc.scalar.activation(gate[:, n, :], r_bank[u][half][:, n, :], SIGMOID, bias=bias_sb[:, t : t + 1])
-                for n in range(2):
-                    cols = slice(n * QUARTER, (n + 1) * QUARTER)
-                    nc.vector.scalar_tensor_tensor(
-                        result[:, :, cols], gate[:, :, cols], 1.0, y_bank[2 * half + n][:, 2 * u : 2 * u + 2, :], ADD, MULT
-                    )
-                nc.sync.dma_start(out_rows[:, 2 * u : 2 * u + 2, half * HALF : (half + 1) * HALF], result[:])
+
+        def gates(u, half):
+            gate = sb("gate%d_%d" % (u, half), [P, 2, HALF], F32)
+            for n in range(2):
+                rows = slice(n * P, (n + 1) * P)
+                r_bank = psum.tile([P, HALF], F32, name="r_bank%d_%d" % (n, u))
+                nc.tensor.matmul_mx(
+                    out=r_bank[:],
+                    lhsT=w3_codes[u][:, rows].bitcast(FP8X4),
+                    lhsT_scale=w3_scale[u][:, rows],
+                    rhs=y_codes[half][:].bitcast(FP8X4),
+                    rhs_scale=y_scale[half][:],
+                    start=True,
+                    stop=True,
+                )
+                t = 2 * u + n
+                nc.scalar.activation(gate[:, n, :], r_bank[:], SIGMOID, bias=bias_sb[:, t : t + 1])
+            return gate
+
+        def finish(gate, u, half, first, count):
+            tiles = slice(2 * u + first, 2 * u + first + count)
+            result = sb("result%d_%d_%d" % (u, half, first), [P, count, HALF], F32)
+            for n in range(2):
+                cols = slice(n * QUARTER, (n + 1) * QUARTER)
+                nc.vector.scalar_tensor_tensor(
+                    result[:, :, cols], gate[:, first : first + count, cols], 1.0, y_bank[2 * half + n][:, tiles, :], ADD, MULT
+                )
+            nc.sync.dma_start(out_rows[:, tiles, half * HALF : (half + 1) * HALF], result[:])
+
+        for half in range(2):
+            for u in range(2):
+                gate = gates(u, half)
+                if u == half:
+                    finish(gate, u, half, 0, 1)
+                    finish(gate, u, half, 1, 1)
+                else:
+                    finish(gate, u, half, 0, 2)

@@ -21,7 +21,7 @@ PACK = 4
 QUARTER = S // PACK
 HALF = S // 2
 SPREAD = 8
-W_VECTOR_M = (32, 64)
+W_VECTOR_M = (64, 96)
 
 
 def tile_picked_ydcn_gate_p_kernel(
@@ -139,8 +139,10 @@ def tile_picked_ydcn_gate_p_kernel(
         for q in range(PACK):
             for t in range(PACK):
                 first_pass(1, e_codes, q, t)
-            turned = y_bank[q][:].rearrange("p t n -> p n t")
-            nc.scalar.copy(y_bf[q // 2][:, q % 2], turned)
+            nc.scalar.copy(
+                y_bf[q // 2][:, q % 2].rearrange("p (n i) t -> p n t i", i=2),
+                y_bank[q][:].rearrange("p t (n i) -> p n t i", i=2),
+            )
 
         def quantize_y(half):
             nc.vector.quantize_mx(
@@ -207,7 +209,7 @@ def tile_picked_ydcn_gate_p_kernel(
         for half in range(2):
             for u in range(2):
                 gate = gates(u, half)
-                if u == half:
+                if half == 0:
                     finish(gate, u, half, 0, 1)
                     finish(gate, u, half, 1, 1)
                 else:

@@ -2,7 +2,7 @@ from contextlib import ExitStack
 
 import concourse.mybir as mybir
 
-K, T, S, H = 512, 2048, 512, 512
+T, S, H = 2048, 512, 512
 FLOPS = 3 * 2 * 512 * 512 * 512
 
 F32 = mybir.dt.float32
@@ -20,6 +20,8 @@ P = 128
 PACK = 4
 QUARTER = S // PACK
 HALF = S // 2
+LIST_HALF = HALF // 16
+QUADRANT = 32
 SPREAD = 8
 W_VECTOR_M = (64, 96)
 
@@ -45,15 +47,15 @@ def tile_picked_ydcn_gate_p_kernel(
         w3_raw = [sb("w3_raw%d" % side, [P, PACK, H // 2], F32) for side in range(2)]
         bias_sb = sb("bias_sb", [P, PACK], F32)
 
-        warm_in = sb("warm_in", [P, 1], F32)
-        warm_out = sb("warm_out", [P, 1], F32)
+        preload_in = sb("preload_in", [P, 1], F32)
+        preload_out = sb("preload_out", [P, 1], F32)
         picked_scale = sb("picked_scale", [P, 2 * S], U8)
         scale = sb("scale", [P, 2 * S], U8)
         nc.vector.memset(x_scale_table[:].bitcast(I32), 0)
         nc.vector.memset(e_scale_table[:].bitcast(I32), 0)
-        nc.vector.memset(warm_in[:], 0.0)
+        nc.vector.memset(preload_in[:], 0.0)
         nc.vector.memset(scale[:].bitcast(I32), 0)
-        nc.scalar.activation(warm_out[:], warm_in[:], SIGMOID)
+        nc.scalar.activation(preload_out[:], preload_in[:], SIGMOID)
 
         def load_weight(n, w, rows):
             nc.sync.dma_start(w_raw[n][:, rows], w.rearrange("(p j) c -> p j c", j=PACK)[:, rows])
@@ -74,8 +76,10 @@ def tile_picked_ydcn_gate_p_kernel(
         load_weight(1, w2, slice(0, 4))
         nc.vector.tensor_copy(picked_scale[:, :S], x_scale_table[:].indirect(offs_list[:]))
         nc.vector.tensor_copy(picked_scale[:, S:], e_scale_table[:].indirect(item_list[:]))
-        for r in range(4):
-            nc.sync.dma_start(scale[r:P:32, :].bitcast(I32), picked_scale[SPREAD * r : P : 32, :].bitcast(I32))
+        for r in range(PACK):
+            nc.sync.dma_start(
+                scale[r:P:QUADRANT, :].bitcast(I32), picked_scale[SPREAD * r : P : QUADRANT, :].bitcast(I32)
+            )
         load_words(e_table, e_words)
         for side in range(2):
             cols = slice(side * (H // 2), (side + 1) * (H // 2))
@@ -120,8 +124,12 @@ def tile_picked_ydcn_gate_p_kernel(
                 stop=(n == 1 and t == PACK - 1),
             )
 
-        for half in range(2):
-            nc.vector.tensor_copy(x_codes[half][:], x_table[:].indirect(offs_list[:, 16 * half : 16 * half + 16]))
+        def gather_words(codes, table, entries):
+            for half in range(2):
+                part = entries[:, half * LIST_HALF : (half + 1) * LIST_HALF]
+                nc.vector.tensor_copy(codes[half][:], table[:].indirect(part))
+
+        gather_words(x_codes, x_table, offs_list)
         for q in range(PACK):
             for t in range(PACK):
                 first_pass(0, x_codes, q, t)
@@ -129,8 +137,7 @@ def tile_picked_ydcn_gate_p_kernel(
         cast_weight(1)
         quantize_weight(1)
 
-        for half in range(2):
-            nc.vector.tensor_copy(e_codes[half][:], e_table[:].indirect(item_list[:, 16 * half : 16 * half + 16]))
+        gather_words(e_codes, e_table, item_list)
 
         y_bf = [sb("y_bf%d" % half, [P, 2, QUARTER, PACK], BF16) for half in range(2)]
         y_codes = [sb("y_codes%d" % half, [P, HALF], U32) for half in range(2)]
@@ -177,12 +184,11 @@ def tile_picked_ydcn_gate_p_kernel(
         quantize_y(1)
 
         out_rows = out.rearrange("(p t) j -> p t j", t=PACK)
-
-        def gates(u, half):
-            gate = sb("gate%d_%d" % (u, half), [P, 2, HALF], F32)
-            for n in range(2):
-                rows = slice(n * P, (n + 1) * P)
-                r_bank = psum.tile([P, HALF], F32, name="r_bank%d_%d" % (n, u))
+        for half in range(2):
+            for t in range(PACK):
+                u, place = divmod(t, 2)
+                rows = slice(place * P, (place + 1) * P)
+                r_bank = psum.tile([P, HALF], F32, name="r_bank%d" % t)
                 nc.tensor.matmul_mx(
                     out=r_bank[:],
                     lhsT=w3_codes[u][:, rows].bitcast(FP8X4),
@@ -192,25 +198,10 @@ def tile_picked_ydcn_gate_p_kernel(
                     start=True,
                     stop=True,
                 )
-                t = 2 * u + n
-                nc.scalar.activation(gate[:, n, :], r_bank[:], SIGMOID, bias=bias_sb[:, t : t + 1])
-            return gate
-
-        def finish(gate, u, half, first, count):
-            tiles = slice(2 * u + first, 2 * u + first + count)
-            result = sb("result%d_%d_%d" % (u, half, first), [P, count, HALF], F32)
-            for n in range(2):
-                cols = slice(n * QUARTER, (n + 1) * QUARTER)
-                nc.vector.scalar_tensor_tensor(
-                    result[:, :, cols], gate[:, first : first + count, cols], 1.0, y_bank[2 * half + n][:, tiles, :], ADD, MULT
-                )
-            nc.sync.dma_start(out_rows[:, tiles, half * HALF : (half + 1) * HALF], result[:])
-
-        for half in range(2):
-            for u in range(2):
-                gate = gates(u, half)
-                if half == 0:
-                    finish(gate, u, half, 0, 1)
-                    finish(gate, u, half, 1, 1)
-                else:
-                    finish(gate, u, half, 0, 2)
+                gate = sb("gate%d_%d" % (t, half), [P, HALF], F32)
+                nc.scalar.activation(gate[:], r_bank[:], SIGMOID, bias=bias_sb[:, t : t + 1])
+                result = sb("result%d_%d" % (t, half), [P, HALF], F32)
+                for q in range(2 * half, 2 * half + 2):
+                    cols = slice((q % 2) * QUARTER, (q % 2 + 1) * QUARTER)
+                    nc.vector.scalar_tensor_tensor(result[:, cols], gate[:, cols], 1.0, y_bank[q][:, t, :], ADD, MULT)
+                nc.sync.dma_start(out_rows[:, t, half * HALF : (half + 1) * HALF], result[:])

@@ -24,6 +24,7 @@ LIST_HALF = HALF // 16
 QUADRANT = 32
 SPREAD = 8
 W_VECTOR_M = (64, 96)
+W3_SIDES = (slice(0, 64), slice(64, 96), slice(96, P))
 
 
 def tile_picked_ydcn_gate_p_kernel(
@@ -44,7 +45,7 @@ def tile_picked_ydcn_gate_p_kernel(
         x_scale_table = sb("x_scale_table", [P, T], U8)
         e_scale_table = sb("e_scale_table", [P, T], U8)
         w_raw = [sb("w_raw%d" % n, [P, PACK, H], F32) for n in range(2)]
-        w3_raw = [sb("w3_raw%d" % side, [P, PACK, H // 2], F32) for side in range(2)]
+        w3_raw = [sb("w3_raw%d" % side, [P, PACK, PACK * (ms.stop - ms.start)], F32) for side, ms in enumerate(W3_SIDES)]
         bias_sb = sb("bias_sb", [P, PACK], F32)
 
         preload_in = sb("preload_in", [P, 1], F32)
@@ -54,7 +55,6 @@ def tile_picked_ydcn_gate_p_kernel(
         nc.vector.memset(x_scale_table[:].bitcast(I32), 0)
         nc.vector.memset(e_scale_table[:].bitcast(I32), 0)
         nc.vector.memset(preload_in[:], 0.0)
-        nc.vector.memset(scale[:].bitcast(I32), 0)
         nc.scalar.activation(preload_out[:], preload_in[:], SIGMOID)
 
         def load_weight(n, w, rows):
@@ -76,13 +76,14 @@ def tile_picked_ydcn_gate_p_kernel(
         load_weight(1, w2, slice(0, 4))
         nc.vector.tensor_copy(picked_scale[:, :S], x_scale_table[:].indirect(offs_list[:]))
         nc.vector.tensor_copy(picked_scale[:, S:], e_scale_table[:].indirect(item_list[:]))
-        for r in range(PACK):
+        nc.vector.tensor_copy(scale[:].bitcast(I32), picked_scale[:].bitcast(I32))
+        for r in range(1, PACK):
             nc.sync.dma_start(
                 scale[r:P:QUADRANT, :].bitcast(I32), picked_scale[SPREAD * r : P : QUADRANT, :].bitcast(I32)
             )
         load_words(e_table, e_words)
-        for side in range(2):
-            cols = slice(side * (H // 2), (side + 1) * (H // 2))
+        for side in range(len(W3_SIDES)):
+            cols = slice(PACK * W3_SIDES[side].start, PACK * W3_SIDES[side].stop)
             nc.sync.dma_start(w3_raw[side][:], w3.rearrange("(p j) c -> p j c", j=PACK)[:, :, cols])
         nc.sync.dma_start(bias_sb[:], bias.rearrange("(p t) o -> p (t o)", t=PACK))
 
@@ -139,67 +140,89 @@ def tile_picked_ydcn_gate_p_kernel(
 
         gather_words(e_codes, e_table, item_list)
 
-        y_bf = [sb("y_bf%d" % half, [P, 2, QUARTER, PACK], BF16) for half in range(2)]
+        y_parts = (slice(0, 128), slice(128, 256), slice(256, 320), slice(320, 384), slice(384, 512))
         y_codes = [sb("y_codes%d" % half, [P, HALF], U32) for half in range(2)]
-        w3_bf = [sb("w3_bf%d" % u, [P, 2, P, PACK], BF16) for u in range(2)]
-        y_scale = []
+        y_scale = {}
+        y_bf = {}
+        w3_bf = sb("w3_bf", [P, PACK, P, PACK], BF16)
+
+        def round_y(copy, part, entries):
+            q, first = divmod(entries.start, QUARTER)
+            width = entries.stop - entries.start
+            place = entries.start - y_parts[part].start
+            copy(
+                y_bf[part][:, place : place + width].rearrange("p (n i) t -> p n t i", i=2),
+                y_bank[q][:, :, first : first + width].rearrange("p t (n i) -> p n t i", i=2),
+            )
+
+        def quantize_y(part):
+            half, first = divmod(y_parts[part].start, HALF)
+            cols = slice(first, first + y_parts[part].stop - y_parts[part].start)
+            nc.vector.quantize_mx(
+                out=y_codes[half][:, cols].bitcast(FP8X4),
+                scales=y_scale[half][:, cols],
+                in_=y_bf[part][:].rearrange("p n t -> p (n t)"),
+            )
+
+        for part in (0, 1, 3, 4):
+            y_bf[part] = sb("y_bf%d" % part, [P, y_parts[part].stop - y_parts[part].start, PACK], BF16)
         for q in range(PACK):
             for t in range(PACK):
                 first_pass(1, e_codes, q, t)
-            nc.scalar.copy(
-                y_bf[q // 2][:, q % 2].rearrange("p (n i) t -> p n t i", i=2),
-                y_bank[q][:].rearrange("p t (n i) -> p n t i", i=2),
-            )
+        for part in (0, 1, 3, 4):
+            round_y(nc.scalar.copy, part, y_parts[part])
 
-        def quantize_y(half):
-            nc.vector.quantize_mx(
-                out=y_codes[half][:].bitcast(FP8X4),
-                scales=y_scale[half][:],
-                in_=y_bf[half][:].rearrange("p q n t -> p (q n t)"),
-            )
-
-        w3_codes = [sb("w3_codes%d" % u, [P, 2 * P], U32) for u in range(2)]
-        w3_scale = [sb("w3_scale%d" % u, [P, 2 * P], U8) for u in range(2)]
+        w3_codes = sb("w3_codes", [P, H], U32)
+        w3_scale = sb("w3_scale", [P, H], U8)
 
         def cast_w3(side, u):
-            dst = w3_bf[u][:].rearrange("p t m j -> p m j t")[:, side * (P // 2) : (side + 1) * (P // 2)]
+            dst = w3_bf[:, 2 * u : 2 * u + 2].rearrange("p t m j -> p m j t")[:, W3_SIDES[side]]
             src = w3_raw[side][:].rearrange("p j (m t) -> p m j t", t=PACK)[:, :, :, 2 * u : 2 * u + 2]
             nc.vector.tensor_copy(dst, src)
 
-        def quantize_w3(u):
+        def quantize_w3(tiles):
+            cols = slice(tiles.start * P, tiles.stop * P)
             nc.vector.quantize_mx(
-                out=w3_codes[u][:].bitcast(FP8X4),
-                scales=w3_scale[u][:],
-                in_=w3_bf[u][:].rearrange("p t m j -> p (t m j)"),
+                out=w3_codes[:, cols].bitcast(FP8X4),
+                scales=w3_scale[:, cols],
+                in_=w3_bf[:, tiles].rearrange("p t m j -> p (t m j)"),
             )
 
-        for side in range(2):
+        for side in range(len(W3_SIDES)):
             for u in range(2):
                 cast_w3(side, u)
-        quantize_w3(0)
-        y_scale.append(sb("y_scale0", [P, HALF], U8, "w3_raw1"))
+        quantize_w3(slice(0, 1))
+        y_scale[0] = sb("y_scale0", [P, HALF], U8, "w3_raw2")
         quantize_y(0)
-        quantize_w3(1)
-        y_scale.append(sb("y_scale1", [P, HALF], U8, "y_bf0"))
         quantize_y(1)
+        quantize_w3(slice(1, 3))
+        quantize_w3(slice(3, 4))
+        y_bf[2] = sb("y_bf2", [P, 64, PACK], BF16, "y_bf1")
+        round_y(nc.vector.tensor_copy, 2, y_parts[2])
+        y_scale[1] = sb("y_scale1", [P, HALF], U8, "w3_bf")
+        for part in (3, 4, 2):
+            quantize_y(part)
 
         out_rows = out.rearrange("(p t) j -> p t j", t=PACK)
         for half in range(2):
             for t in range(PACK):
-                u, place = divmod(t, 2)
-                rows = slice(place * P, (place + 1) * P)
-                r_bank = psum.tile([P, HALF], F32, name="r_bank%d" % t)
-                nc.tensor.matmul_mx(
-                    out=r_bank[:],
-                    lhsT=w3_codes[u][:, rows].bitcast(FP8X4),
-                    lhsT_scale=w3_scale[u][:, rows],
-                    rhs=y_codes[half][:].bitcast(FP8X4),
-                    rhs_scale=y_scale[half][:],
-                    start=True,
-                    stop=True,
-                )
+                rows = slice(t * P, (t + 1) * P)
                 gate = sb("gate%d_%d" % (t, half), [P, HALF], F32)
-                nc.scalar.activation(gate[:], r_bank[:], SIGMOID, bias=bias_sb[:, t : t + 1])
+                spans = [(t, slice(0, HALF))]
+                if half == 0 and t == 0:
+                    spans = [(0, slice(0, QUARTER)), (PACK - 1, slice(QUARTER, HALF))]
+                for bank, span in spans:
+                    r_bank = psum.tile([P, HALF], F32, name="r_bank%d" % bank)
+                    nc.tensor.matmul_mx(
+                        out=r_bank[:, span],
+                        lhsT=w3_codes[:, rows].bitcast(FP8X4),
+                        lhsT_scale=w3_scale[:, rows],
+                        rhs=y_codes[half][:, span].bitcast(FP8X4),
+                        rhs_scale=y_scale[half][:, span],
+                        start=True,
+                        stop=True,
+                    )
+                    nc.scalar.activation(gate[:, span], r_bank[:, span], SIGMOID, bias=bias_sb[:, t : t + 1])
                 result = sb("result%d_%d" % (t, half), [P, HALF], F32)
                 for q in range(2 * half, 2 * half + 2):
                     cols = slice((q % 2) * QUARTER, (q % 2 + 1) * QUARTER)

@@ -24,7 +24,10 @@ LIST_HALF = HALF // 16
 QUADRANT = 32
 SPREAD = 8
 W_VECTOR_M = (64, 96)
-W3_SIDES = (slice(0, 64), slice(64, 96), slice(96, P))
+W3_LOADS = (slice(0, 64), slice(64, 96), slice(96, P))
+Y_RANGES = (slice(0, 128), slice(128, 256), slice(256, 320), slice(320, 384), slice(384, 512))
+Y_ON_SCALAR = (0, 1, 3, 4)
+Y_ON_VECTOR = 2
 
 
 def tile_picked_ydcn_gate_p_kernel(
@@ -45,7 +48,7 @@ def tile_picked_ydcn_gate_p_kernel(
         x_scale_table = sb("x_scale_table", [P, T], U8)
         e_scale_table = sb("e_scale_table", [P, T], U8)
         w_raw = [sb("w_raw%d" % n, [P, PACK, H], F32) for n in range(2)]
-        w3_raw = [sb("w3_raw%d" % side, [P, PACK, PACK * (ms.stop - ms.start)], F32) for side, ms in enumerate(W3_SIDES)]
+        w3_raw = [sb("w3_raw%d" % n, [P, PACK, PACK * (ms.stop - ms.start)], F32) for n, ms in enumerate(W3_LOADS)]
         bias_sb = sb("bias_sb", [P, PACK], F32)
 
         preload_in = sb("preload_in", [P, 1], F32)
@@ -82,9 +85,9 @@ def tile_picked_ydcn_gate_p_kernel(
                 scale[r:P:QUADRANT, :].bitcast(I32), picked_scale[SPREAD * r : P : QUADRANT, :].bitcast(I32)
             )
         load_words(e_table, e_words)
-        for side in range(len(W3_SIDES)):
-            cols = slice(PACK * W3_SIDES[side].start, PACK * W3_SIDES[side].stop)
-            nc.sync.dma_start(w3_raw[side][:], w3.rearrange("(p j) c -> p j c", j=PACK)[:, :, cols])
+        for n, ms in enumerate(W3_LOADS):
+            cols = slice(PACK * ms.start, PACK * ms.stop)
+            nc.sync.dma_start(w3_raw[n][:], w3.rearrange("(p j) c -> p j c", j=PACK)[:, :, cols])
         nc.sync.dma_start(bias_sb[:], bias.rearrange("(p t) o -> p (t o)", t=PACK))
 
         w_bf = [sb("w_bf%d" % n, [P, PACK, P, PACK], BF16) for n in range(2)]
@@ -140,91 +143,97 @@ def tile_picked_ydcn_gate_p_kernel(
 
         gather_words(e_codes, e_table, item_list)
 
-        y_parts = (slice(0, 128), slice(128, 256), slice(256, 320), slice(320, 384), slice(384, 512))
         y_codes = [sb("y_codes%d" % half, [P, HALF], U32) for half in range(2)]
         y_scale = {}
         y_bf = {}
         w3_bf = sb("w3_bf", [P, PACK, P, PACK], BF16)
 
-        def round_y(copy, part, entries):
-            q, first = divmod(entries.start, QUARTER)
-            width = entries.stop - entries.start
-            place = entries.start - y_parts[part].start
+        def round_y(copy, n):
+            q, first = divmod(Y_RANGES[n].start, QUARTER)
+            within = slice(first, first + Y_RANGES[n].stop - Y_RANGES[n].start)
             copy(
-                y_bf[part][:, place : place + width].rearrange("p (n i) t -> p n t i", i=2),
-                y_bank[q][:, :, first : first + width].rearrange("p t (n i) -> p n t i", i=2),
+                y_bf[n][:].rearrange("p (e i) t -> p e t i", i=2),
+                y_bank[q][:, :, within].rearrange("p t (e i) -> p e t i", i=2),
             )
 
-        def quantize_y(part):
-            half, first = divmod(y_parts[part].start, HALF)
-            cols = slice(first, first + y_parts[part].stop - y_parts[part].start)
+        def quantize_y(n):
+            half, first = divmod(Y_RANGES[n].start, HALF)
+            cols = slice(first, first + Y_RANGES[n].stop - Y_RANGES[n].start)
             nc.vector.quantize_mx(
                 out=y_codes[half][:, cols].bitcast(FP8X4),
                 scales=y_scale[half][:, cols],
-                in_=y_bf[part][:].rearrange("p n t -> p (n t)"),
+                in_=y_bf[n][:].rearrange("p e t -> p (e t)"),
             )
 
-        for part in (0, 1, 3, 4):
-            y_bf[part] = sb("y_bf%d" % part, [P, y_parts[part].stop - y_parts[part].start, PACK], BF16)
+        for n in Y_ON_SCALAR:
+            y_bf[n] = sb("y_bf%d" % n, [P, Y_RANGES[n].stop - Y_RANGES[n].start, PACK], BF16)
         for q in range(PACK):
             for t in range(PACK):
                 first_pass(1, e_codes, q, t)
-        for part in (0, 1, 3, 4):
-            round_y(nc.scalar.copy, part, y_parts[part])
+        for n in Y_ON_SCALAR:
+            round_y(nc.scalar.copy, n)
 
         w3_codes = sb("w3_codes", [P, H], U32)
         w3_scale = sb("w3_scale", [P, H], U8)
 
-        def cast_w3(side, u):
-            dst = w3_bf[:, 2 * u : 2 * u + 2].rearrange("p t m j -> p m j t")[:, W3_SIDES[side]]
-            src = w3_raw[side][:].rearrange("p j (m t) -> p m j t", t=PACK)[:, :, :, 2 * u : 2 * u + 2]
-            nc.vector.tensor_copy(dst, src)
+        def cast_w3(n):
+            for pair in (slice(0, 2), slice(2, 4)):
+                dst = w3_bf[:, pair].rearrange("p t m j -> p m j t")[:, W3_LOADS[n]]
+                src = w3_raw[n][:].rearrange("p j (m t) -> p m j t", t=PACK)[:, :, :, pair]
+                nc.vector.tensor_copy(dst, src)
 
-        def quantize_w3(tiles):
-            cols = slice(tiles.start * P, tiles.stop * P)
+        def quantize_w3(cols):
             nc.vector.quantize_mx(
                 out=w3_codes[:, cols].bitcast(FP8X4),
                 scales=w3_scale[:, cols],
-                in_=w3_bf[:, tiles].rearrange("p t m j -> p (t m j)"),
+                in_=w3_bf[:].rearrange("p t m j -> p (t m j)")[:, PACK * cols.start : PACK * cols.stop],
             )
 
-        for side in range(len(W3_SIDES)):
-            for u in range(2):
-                cast_w3(side, u)
-        quantize_w3(slice(0, 1))
+        cast_w3(0)
+        for t in range(2):
+            quantize_w3(slice(t * P, t * P + P // 2))
+        cast_w3(1)
+        cast_w3(2)
+        for t in range(2):
+            quantize_w3(slice(t * P + P // 2, (t + 1) * P))
         y_scale[0] = sb("y_scale0", [P, HALF], U8, "w3_raw2")
         quantize_y(0)
         quantize_y(1)
-        quantize_w3(slice(1, 3))
-        quantize_w3(slice(3, 4))
-        y_bf[2] = sb("y_bf2", [P, 64, PACK], BF16, "y_bf1")
-        round_y(nc.vector.tensor_copy, 2, y_parts[2])
+        quantize_w3(slice(2 * P, 4 * P))
+        y_bf[Y_ON_VECTOR] = sb("y_bf2", [P, QUARTER // 2, PACK], BF16, "y_bf1")
+        round_y(nc.vector.tensor_copy, Y_ON_VECTOR)
         y_scale[1] = sb("y_scale1", [P, HALF], U8, "w3_bf")
-        for part in (3, 4, 2):
-            quantize_y(part)
+        for n in (3, 4, Y_ON_VECTOR):
+            quantize_y(n)
+
+        def second_product(t, half, bank, cols):
+            rows = slice(t * P, (t + 1) * P)
+            r_bank = psum.tile([P, HALF], F32, name="r_bank%d" % bank)
+            nc.tensor.matmul_mx(
+                out=r_bank[:, cols],
+                lhsT=w3_codes[:, rows].bitcast(FP8X4),
+                lhsT_scale=w3_scale[:, rows],
+                rhs=y_codes[half][:, cols].bitcast(FP8X4),
+                rhs_scale=y_scale[half][:, cols],
+                start=True,
+                stop=True,
+            )
+            return r_bank
 
         out_rows = out.rearrange("(p t) j -> p t j", t=PACK)
-        for half in range(2):
-            for t in range(PACK):
-                rows = slice(t * P, (t + 1) * P)
-                gate = sb("gate%d_%d" % (t, half), [P, HALF], F32)
-                spans = [(t, slice(0, HALF))]
-                if half == 0 and t == 0:
-                    spans = [(0, slice(0, QUARTER)), (PACK - 1, slice(QUARTER, HALF))]
-                for bank, span in spans:
-                    r_bank = psum.tile([P, HALF], F32, name="r_bank%d" % bank)
-                    nc.tensor.matmul_mx(
-                        out=r_bank[:, span],
-                        lhsT=w3_codes[:, rows].bitcast(FP8X4),
-                        lhsT_scale=w3_scale[:, rows],
-                        rhs=y_codes[half][:, span].bitcast(FP8X4),
-                        rhs_scale=y_scale[half][:, span],
-                        start=True,
-                        stop=True,
-                    )
-                    nc.scalar.activation(gate[:, span], r_bank[:, span], SIGMOID, bias=bias_sb[:, t : t + 1])
-                result = sb("result%d_%d" % (t, half), [P, HALF], F32)
-                for q in range(2 * half, 2 * half + 2):
-                    cols = slice((q % 2) * QUARTER, (q % 2 + 1) * QUARTER)
-                    nc.vector.scalar_tensor_tensor(result[:, cols], gate[:, cols], 1.0, y_bank[q][:, t, :], ADD, MULT)
-                nc.sync.dma_start(out_rows[:, t, half * HALF : (half + 1) * HALF], result[:])
+        quarters = (slice(0, QUARTER), slice(QUARTER, HALF))
+        pieces = [(half, t) for half in range(2) for t in range(PACK)]
+        for half, t in pieces:
+            gate = sb("gate%d_%d" % (t, half), [P, HALF], F32)
+            if (half, t) == pieces[0]:
+                for bank, cols in zip((t, PACK - 1), quarters):
+                    r_bank = second_product(t, half, bank, cols)
+                    nc.scalar.activation(gate[:, cols], r_bank[:, cols], SIGMOID, bias=bias_sb[:, t : t + 1])
+            else:
+                r_bank = second_product(t, half, t, slice(0, HALF))
+                for cols in quarters if (half, t) in (pieces[1], pieces[-1]) else (slice(0, HALF),):
+                    nc.scalar.activation(gate[:, cols], r_bank[:, cols], SIGMOID, bias=bias_sb[:, t : t + 1])
+            result = sb("result%d_%d" % (t, half), [P, HALF], F32)
+            for q, cols in enumerate(quarters, 2 * half):
+                nc.vector.scalar_tensor_tensor(result[:, cols], gate[:, cols], 1.0, y_bank[q][:, t, :], ADD, MULT)
+            nc.sync.dma_start(out_rows[:, t, half * HALF : (half + 1) * HALF], result[:])

@@ -226,11 +226,11 @@ def tile_picked_ydcn_gate_p_kernel(
         for half, t in pieces:
             gate = sb("gate%d_%d" % (t, half), [P, HALF], F32)
             if (half, t) == pieces[0]:
-                for bank, cols in zip((t, PACK - 1), quarters):
+                for bank, cols in enumerate(quarters):
                     r_bank = second_product(t, half, bank, cols)
                     nc.scalar.activation(gate[:, cols], r_bank[:, cols], SIGMOID, bias=bias_sb[:, t : t + 1])
             else:
-                r_bank = second_product(t, half, t, slice(0, HALF))
+                r_bank = second_product(t, half, (PACK * half + t + 1) % PACK, slice(0, HALF))
                 for cols in quarters if (half, t) in (pieces[1], pieces[-1]) else (slice(0, HALF),):
                     nc.scalar.activation(gate[:, cols], r_bank[:, cols], SIGMOID, bias=bias_sb[:, t : t + 1])
             result = sb("result%d_%d" % (t, half), [P, HALF], F32)

@@ -25,9 +25,8 @@ QUADRANT = 32
 SPREAD = 8
 W_VECTOR_M = (64, 96)
 W3_LOADS = (slice(0, 64), slice(64, 96), slice(96, P))
-Y_RANGES = (slice(0, 128), slice(128, 256), slice(256, 320), slice(320, 384), slice(384, 512))
-Y_ON_SCALAR = (0, 1, 3, 4)
-Y_ON_VECTOR = 2
+Y_RANGES = tuple(slice(q * QUARTER, (q + 1) * QUARTER) for q in range(PACK))
+Y_ON_SCALAR = (0, 1, 2, 3)
 
 
 def tile_picked_ydcn_gate_p_kernel(
@@ -200,10 +199,8 @@ def tile_picked_ydcn_gate_p_kernel(
         quantize_y(0)
         quantize_y(1)
         quantize_w3(slice(2 * P, 4 * P))
-        y_bf[Y_ON_VECTOR] = sb("y_bf2", [P, QUARTER // 2, PACK], BF16, "y_bf1")
-        round_y(nc.vector.tensor_copy, Y_ON_VECTOR)
         y_scale[1] = sb("y_scale1", [P, HALF], U8, "w3_bf")
-        for n in (3, 4, Y_ON_VECTOR):
+        for n in (2, 3):
             quantize_y(n)
 
         def second_product(t, half, bank, cols):

@@ -199,7 +199,7 @@ def tile_picked_ydcn_gate_p_kernel(
         quantize_y(0)
         quantize_y(1)
         quantize_w3(slice(2 * P, 4 * P))
-        y_scale[1] = sb("y_scale1", [P, HALF], U8, "w3_bf")
+        y_scale[1] = sb("y_scale1", [P, HALF], U8, "y_bf0")
         for n in (2, 3):
             quantize_y(n)
 

@@ -38,7 +38,7 @@ def tile_picked_ydcn_gate_p_kernel(
         psum = ctx.enter_context(tc.psum_pool(name="psum", bufs=1))
 
         def sb(name, shape, dtype, tag=None):
-            return keep.tile(shape, dtype, name=name, tag=tag or name, align_bytes=64)
+            return keep.tile(shape, dtype, name=name, tag=tag or name, align_bytes=256)
 
         offs_list = keep.tile([P, S // 16], U16, name="offs_list")
         item_list = keep.tile([P, S // 16], U16, name="item_list")

@@ -24,7 +24,8 @@ LIST_HALF = HALF // 16
 QUADRANT = 32
 SPREAD = 8
 W_VECTOR_M = (64, 96)
-W3_LOADS = (slice(0, 64), slice(64, 96), slice(96, P))
+W3_LOADS = (slice(0, 32), slice(32, 96), slice(96, P))
+ITEM_PARTS = (slice(0, 8), slice(8, 16), slice(16, 32))
 Y_RANGES = tuple(slice(q * QUARTER, (q + 1) * QUARTER) for q in range(PACK))
 Y_ON_SCALAR = (0, 1, 2, 3)
 
@@ -140,7 +141,10 @@ def tile_picked_ydcn_gate_p_kernel(
         cast_weight(1)
         quantize_weight(1)
 
-        gather_words(e_codes, e_table, item_list)
+        for part in ITEM_PARTS:
+            half, first = divmod(16 * part.start, HALF)
+            cols = slice(first, first + 16 * (part.stop - part.start))
+            nc.vector.tensor_copy(e_codes[half][:, cols], e_table[:].indirect(item_list[:, part]))
 
         y_codes = [sb("y_codes%d" % half, [P, HALF], U32) for half in range(2)]
         y_scale = {}
@@ -188,16 +192,12 @@ def tile_picked_ydcn_gate_p_kernel(
                 in_=w3_bf[:].rearrange("p t m j -> p (t m j)")[:, PACK * cols.start : PACK * cols.stop],
             )
 
-        cast_w3(0)
-        for t in range(2):
-            quantize_w3(slice(t * P, t * P + P // 2))
-        cast_w3(1)
-        cast_w3(2)
-        for t in range(2):
-            quantize_w3(slice(t * P + P // 2, (t + 1) * P))
-        y_scale[0] = sb("y_scale0", [P, HALF], U8, "w3_raw2")
-        quantize_y(0)
-        quantize_y(1)
+        for n in range(len(W3_LOADS)):
+            cast_w3(n)
+        y_scale[0] = sb("y_scale0", [P, HALF], U8, "w3_raw1")
+        for n in range(2):
+            quantize_y(n)
+            quantize_w3(slice(n * P, (n + 1) * P))
         quantize_w3(slice(2 * P, 4 * P))
         y_scale[1] = sb("y_scale1", [P, HALF], U8, "y_bf0")
         for n in (2, 3):

@@ -55,8 +55,10 @@ def tile_picked_ydcn_gate_p_kernel(
         preload_out = sb("preload_out", [P, 1], F32)
         picked_scale = sb("picked_scale", [P, 2 * S], U8)
         scale = sb("scale", [P, 2 * S], U8)
-        nc.vector.memset(x_scale_table[:].bitcast(I32), 0)
-        nc.vector.memset(e_scale_table[:].bitcast(I32), 0)
+        for part in range(2):
+            nc.vector.memset(x_scale_table[:, part * 2 * S : (part + 1) * 2 * S].bitcast(I32), 0)
+        for part in range(PACK):
+            nc.vector.memset(e_scale_table[:, part * S : (part + 1) * S].bitcast(I32), 0)
         nc.vector.memset(preload_in[:], 0.0)
         nc.scalar.activation(preload_out[:], preload_in[:], SIGMOID)
 
@@ -100,18 +102,20 @@ def tile_picked_ydcn_gate_p_kernel(
             nc.vector.tensor_copy(dst[:, : W_VECTOR_M[n]], src[:, : W_VECTOR_M[n]])
             nc.scalar.copy(dst[:, W_VECTOR_M[n] :], src[:, W_VECTOR_M[n] :])
 
-        def quantize_weight(n):
-            nc.vector.quantize_mx(
-                out=w_codes[n][:].bitcast(FP8X4),
-                scales=w_scale[n][:],
-                in_=w_bf[n][:].rearrange("p t m j -> p (t m j)"),
-            )
+        def quantize_weight(n, parts):
+            width = H // parts
+            for first in range(0, H, width):
+                nc.vector.quantize_mx(
+                    out=w_codes[n][:, first : first + width].bitcast(FP8X4),
+                    scales=w_scale[n][:, first : first + width],
+                    in_=w_bf[n][:].rearrange("p t m j -> p (t m j)")[:, PACK * first : PACK * (first + width)],
+                )
 
         x_codes = [sb("x_codes%d" % half, [P, HALF], U32) for half in range(2)]
         e_codes = [sb("e_codes%d" % half, [P, HALF], U32) for half in range(2)]
 
         cast_weight(0)
-        quantize_weight(0)
+        quantize_weight(0, PACK)
 
         y_bank = [psum.tile([P, PACK, QUARTER], F32, name="y_bank%d" % q) for q in range(PACK)]
 
@@ -139,7 +143,7 @@ def tile_picked_ydcn_gate_p_kernel(
                 first_pass(0, x_codes, q, t)
 
         cast_weight(1)
-        quantize_weight(1)
+        quantize_weight(1, 1)
 
         for part in ITEM_PARTS:
             half, first = divmod(16 * part.start, HALF)

@@ -115,7 +115,7 @@ def tile_picked_ydcn_gate_p_kernel(
         e_codes = [sb("e_codes%d" % half, [P, HALF], U32) for half in range(2)]
 
         cast_weight(0)
-        quantize_weight(0, PACK)
+        quantize_weight(0, 2 * PACK)
 
         y_bank = [psum.tile([P, PACK, QUARTER], F32, name="y_bank%d" % q) for q in range(PACK)]
 

from contextlib import ExitStack

import concourse.mybir as mybir

T, S, H = 2048, 512, 512
FLOPS = 3 * 2 * 512 * 512 * 512

F32 = mybir.dt.float32
BF16 = mybir.dt.bfloat16
I32 = mybir.dt.int32
U32 = mybir.dt.uint32
U16 = mybir.dt.uint16
U8 = mybir.dt.uint8
FP8X4 = mybir.dt.float8_e4m3fn_x4
SIGMOID = mybir.ActivationFunctionType.Sigmoid
ADD = mybir.AluOpType.add
MULT = mybir.AluOpType.mult

P = 128
PACK = 4
QUARTER = S // PACK
HALF = S // 2
LIST_HALF = HALF // 16
QUADRANT = 32
SPREAD = 8
W_VECTOR_M = (64, 96)
W3_LOADS = (slice(0, 32), slice(32, 96), slice(96, P))
ITEM_PARTS = (slice(0, 8), slice(8, 16), slice(16, 32))
Y_RANGES = tuple(slice(q * QUARTER, (q + 1) * QUARTER) for q in range(PACK))
Y_ON_SCALAR = (0, 1, 2, 3)


def tile_picked_ydcn_gate_p_kernel(
    tc, x_words, x_scales, e_words, e_scales, w1, w2, w3, bias, offs, item, out
):
    nc = tc.nc
    with ExitStack() as ctx:
        keep = ctx.enter_context(tc.tile_pool(name="keep", bufs=1))
        psum = ctx.enter_context(tc.psum_pool(name="psum", bufs=1))

        def sb(name, shape, dtype, tag=None):
            return keep.tile(shape, dtype, name=name, tag=tag or name, align_bytes=256)

        offs_list = keep.tile([P, S // 16], U16, name="offs_list")
        item_list = keep.tile([P, S // 16], U16, name="item_list")
        x_table = sb("x_table", [P, T], U32)
        e_table = sb("e_table", [P, T], U32)
        x_scale_table = sb("x_scale_table", [P, T], U8)
        e_scale_table = sb("e_scale_table", [P, T], U8)
        w_raw = [sb("w_raw%d" % n, [P, PACK, H], F32) for n in range(2)]
        w3_raw = [sb("w3_raw%d" % n, [P, PACK, PACK * (ms.stop - ms.start)], F32) for n, ms in enumerate(W3_LOADS)]
        bias_sb = sb("bias_sb", [P, PACK], F32)

        preload_in = sb("preload_in", [P, 1], F32)
        preload_out = sb("preload_out", [P, 1], F32)
        picked_scale = sb("picked_scale", [P, 2 * S], U8)
        scale = sb("scale", [P, 2 * S], U8)
        for part in range(2):
            nc.vector.memset(x_scale_table[:, part * 2 * S : (part + 1) * 2 * S].bitcast(I32), 0)
        for part in range(PACK):
            nc.vector.memset(e_scale_table[:, part * S : (part + 1) * S].bitcast(I32), 0)
        nc.vector.memset(preload_in[:], 0.0)
        nc.scalar.activation(preload_out[:], preload_in[:], SIGMOID)

        def load_weight(n, w, rows):
            nc.sync.dma_start(w_raw[n][:, rows], w.rearrange("(p j) c -> p j c", j=PACK)[:, rows])

        def load_words(table, words):
            nc.sync.dma_start(table[:].bitcast(I32), words[0].rearrange("p n t -> p (n t)").bitcast(I32))

        def load_scales(table, scales):
            nc.sync.dma_start(table[0:P:SPREAD, :].bitcast(I32), scales[0].bitcast(I32))

        load_weight(0, w1, slice(0, 2))
        nc.sync.dma_start(offs_list[:], offs)
        nc.sync.dma_start(item_list[:], item)
        load_scales(x_scale_table, x_scales)
        load_scales(e_scale_table, e_scales)
        load_weight(0, w1, slice(2, 4))
        load_words(x_table, x_words)
        load_weight(1, w2, slice(0, 4))
        nc.vector.tensor_copy(picked_scale[:, :S], x_scale_table[:].indirect(offs_list[:]))
        nc.vector.tensor_copy(picked_scale[:, S:], e_scale_table[:].indirect(item_list[:]))
        nc.vector.tensor_copy(scale[:].bitcast(I32), picked_scale[:].bitcast(I32))
        for r in range(1, PACK):
            nc.sync.dma_start(
                scale[r:P:QUADRANT, :].bitcast(I32), picked_scale[SPREAD * r : P : QUADRANT, :].bitcast(I32)
            )
        load_words(e_table, e_words)
        for n, ms in enumerate(W3_LOADS):
            cols = slice(PACK * ms.start, PACK * ms.stop)
            nc.sync.dma_start(w3_raw[n][:], w3.rearrange("(p j) c -> p j c", j=PACK)[:, :, cols])
        nc.sync.dma_start(bias_sb[:], bias.rearrange("(p t) o -> p (t o)", t=PACK))

        w_bf = [sb("w_bf%d" % n, [P, PACK, P, PACK], BF16) for n in range(2)]
        w_codes = [sb("w_codes%d" % n, [P, H], U32) for n in range(2)]
        w_scale = [sb("w_scale%d" % n, [P, H], U8) for n in range(2)]

        def cast_weight(n):
            src = w_raw[n][:].rearrange("p j (m t) -> p m t j", t=PACK)
            dst = w_bf[n][:].rearrange("p t m j -> p m t j")
            nc.vector.tensor_copy(dst[:, : W_VECTOR_M[n]], src[:, : W_VECTOR_M[n]])
            nc.scalar.copy(dst[:, W_VECTOR_M[n] :], src[:, W_VECTOR_M[n] :])

        def quantize_weight(n, parts):
            width = H // parts
            for first in range(0, H, width):
                nc.vector.quantize_mx(
                    out=w_codes[n][:, first : first + width].bitcast(FP8X4),
                    scales=w_scale[n][:, first : first + width],
                    in_=w_bf[n][:].rearrange("p t m j -> p (t m j)")[:, PACK * first : PACK * (first + width)],
                )

        x_codes = [sb("x_codes%d" % half, [P, HALF], U32) for half in range(2)]
        e_codes = [sb("e_codes%d" % half, [P, HALF], U32) for half in range(2)]

        cast_weight(0)
        quantize_weight(0, 2 * PACK)

        y_bank = [psum.tile([P, PACK, QUARTER], F32, name="y_bank%d" % q) for q in range(PACK)]

        def first_pass(n, codes, q, t):
            rows = slice(t * P, (t + 1) * P)
            within = slice((q % 2) * QUARTER, (q % 2 + 1) * QUARTER)
            nc.tensor.matmul_mx(
                out=y_bank[q][:, t, :],
                lhsT=w_codes[n][:, rows].bitcast(FP8X4),
                lhsT_scale=w_scale[n][:, rows],
                rhs=codes[q // 2][:, within].bitcast(FP8X4),
                rhs_scale=scale[:, n * S + q * QUARTER : n * S + (q + 1) * QUARTER],
                start=(n == 0 and t == 0),
                stop=(n == 1 and t == PACK - 1),
            )

        def gather_words(codes, table, entries):
            for half in range(2):
                part = entries[:, half * LIST_HALF : (half + 1) * LIST_HALF]
                nc.vector.tensor_copy(codes[half][:], table[:].indirect(part))

        gather_words(x_codes, x_table, offs_list)
        for q in range(PACK):
            for t in range(PACK):
                first_pass(0, x_codes, q, t)

        cast_weight(1)
        quantize_weight(1, 1)

        for part in ITEM_PARTS:
            half, first = divmod(16 * part.start, HALF)
            cols = slice(first, first + 16 * (part.stop - part.start))
            nc.vector.tensor_copy(e_codes[half][:, cols], e_table[:].indirect(item_list[:, part]))

        y_codes = [sb("y_codes%d" % half, [P, HALF], U32) for half in range(2)]
        y_scale = {}
        y_bf = {}
        w3_bf = sb("w3_bf", [P, PACK, P, PACK], BF16)

        def round_y(copy, n):
            q, first = divmod(Y_RANGES[n].start, QUARTER)
            within = slice(first, first + Y_RANGES[n].stop - Y_RANGES[n].start)
            copy(
                y_bf[n][:].rearrange("p (e i) t -> p e t i", i=2),
                y_bank[q][:, :, within].rearrange("p t (e i) -> p e t i", i=2),
            )

        def quantize_y(n):
            half, first = divmod(Y_RANGES[n].start, HALF)
            cols = slice(first, first + Y_RANGES[n].stop - Y_RANGES[n].start)
            nc.vector.quantize_mx(
                out=y_codes[half][:, cols].bitcast(FP8X4),
                scales=y_scale[half][:, cols],
                in_=y_bf[n][:].rearrange("p e t -> p (e t)"),
            )

        for n in Y_ON_SCALAR:
            y_bf[n] = sb("y_bf%d" % n, [P, Y_RANGES[n].stop - Y_RANGES[n].start, PACK], BF16)
        for q in range(PACK):
            for t in range(PACK):
                first_pass(1, e_codes, q, t)
        for n in Y_ON_SCALAR:
            round_y(nc.scalar.copy, n)

        w3_codes = sb("w3_codes", [P, H], U32)
        w3_scale = sb("w3_scale", [P, H], U8)

        def cast_w3(n):
            for pair in (slice(0, 2), slice(2, 4)):
                dst = w3_bf[:, pair].rearrange("p t m j -> p m j t")[:, W3_LOADS[n]]
                src = w3_raw[n][:].rearrange("p j (m t) -> p m j t", t=PACK)[:, :, :, pair]
                nc.vector.tensor_copy(dst, src)

        def quantize_w3(cols):
            nc.vector.quantize_mx(
                out=w3_codes[:, cols].bitcast(FP8X4),
                scales=w3_scale[:, cols],
                in_=w3_bf[:].rearrange("p t m j -> p (t m j)")[:, PACK * cols.start : PACK * cols.stop],
            )

        for n in range(len(W3_LOADS)):
            cast_w3(n)
        y_scale[0] = sb("y_scale0", [P, HALF], U8, "w3_raw1")
        for n in range(2):
            quantize_y(n)
            quantize_w3(slice(n * P, (n + 1) * P))
        quantize_w3(slice(2 * P, 4 * P))
        y_scale[1] = sb("y_scale1", [P, HALF], U8, "y_bf0")
        for n in (2, 3):
            quantize_y(n)

        def second_product(t, half, bank, cols):
            rows = slice(t * P, (t + 1) * P)
            r_bank = psum.tile([P, HALF], F32, name="r_bank%d" % bank)
            nc.tensor.matmul_mx(
                out=r_bank[:, cols],
                lhsT=w3_codes[:, rows].bitcast(FP8X4),
                lhsT_scale=w3_scale[:, rows],
                rhs=y_codes[half][:, cols].bitcast(FP8X4),
                rhs_scale=y_scale[half][:, cols],
                start=True,
                stop=True,
            )
            return r_bank

        out_rows = out.rearrange("(p t) j -> p t j", t=PACK)
        quarters = (slice(0, QUARTER), slice(QUARTER, HALF))
        pieces = [(half, t) for half in range(2) for t in range(PACK)]
        for half, t in pieces:
            gate = sb("gate%d_%d" % (t, half), [P, HALF], F32)
            if (half, t) == pieces[0]:
                for bank, cols in enumerate(quarters):
                    r_bank = second_product(t, half, bank, cols)
                    nc.scalar.activation(gate[:, cols], r_bank[:, cols], SIGMOID, bias=bias_sb[:, t : t + 1])
            else:
                r_bank = second_product(t, half, (PACK * half + t + 1) % PACK, slice(0, HALF))
                for cols in quarters if (half, t) in (pieces[1], pieces[-1]) else (slice(0, HALF),):
                    nc.scalar.activation(gate[:, cols], r_bank[:, cols], SIGMOID, bias=bias_sb[:, t : t + 1])
            result = sb("result%d_%d" % (t, half), [P, HALF], F32)
            for q, cols in enumerate(quarters, 2 * half):
                nc.vector.scalar_tensor_tensor(result[:, cols], gate[:, cols], 1.0, y_bank[q][:, t, :], ADD, MULT)
            nc.sync.dma_start(out_rows[:, t, half * HALF : (half + 1) * HALF], result[:])
